import numpy as np
import ml_dtypes

BF16 = ml_dtypes.bfloat16


def bf(x):
    return np.asarray(x, np.float32).astype(BF16)


def f32(x):
    return np.asarray(x, np.float32)


def f64(x):
    return np.asarray(x).astype(np.float64)


def striped(idx):
    return np.tile(idx.reshape(-1, 16).T, (8, 1))


S, K, M, N, E, Q, O = 512, 128, 384, 128, 2, 64, 256


def gelu_tanh(v):
    return 0.5 * v * (1.0 + np.tanh(np.sqrt(2.0 / np.pi) * (v + 0.044715 * v**3)))


def setup_inputs():
    return {"base": bf(np.random.standard_normal((M, S))), "x": bf(np.random.standard_normal((K, N))), "w": bf(1.2 * np.random.standard_normal((E, K, M)) / np.sqrt(K)), "w2": bf(np.random.standard_normal((M, O)) / np.sqrt(2 * M)), "b": f32(0.5 * np.random.standard_normal((O, 1))), "offs": striped(np.random.permutation(S)[:N])}


def reference(base, x, w, w2, b, offs):
    idx = offs[:16].T.reshape(-1)
    z = f64(base).copy()
    for e in range(E):
        z[:, idx[e * Q : (e + 1) * Q]] += f64(w)[e].T @ f64(x)[:, e * Q : (e + 1) * Q]
    y = f64(w2).T @ z
    return gelu_tanh(y + f64(b))

@@ -1,0 +1,83 @@
+import concourse.mybir as mybir
+from concourse.masks import make_identity
+
+BF16 = mybir.dt.bfloat16
+F32 = mybir.dt.float32
+U16 = mybir.dt.uint16
+GELU_TANH = mybir.ActivationFunctionType.Gelu_apprx_tanh
+
+P = 128
+S = 512
+K = 128
+M = 384
+E = 2
+Q = 64
+N = E * Q
+O = 256
+M_BLOCKS = M // P
+O_BLOCKS = O // P
+LIST_COLUMNS = Q // 16
+
+FLOPS = 2 * K * N * M + 2 * M * O * S
+
+
+def tile_rows_thenproj_gelu_kernel(tc, base, x, w, w2, b, offs, out):
+    nc = tc.nc
+    with (
+        tc.tile_pool(name="held", bufs=1) as held,
+        tc.psum_pool(name="psum", bufs=1) as psum,
+    ):
+        base_sb = held.tile([P, M_BLOCKS, S], BF16, name="base_sb")
+        for m in range(M_BLOCKS):
+            nc.sync.dma_start(base_sb[:, m, :], base[m * P : (m + 1) * P, :])
+        offsets = held.tile([P, N // 16], U16, name="offsets")
+        nc.sync.dma_start(offsets[:], offs)
+        x_sb = held.tile([K, N], BF16, name="x_sb")
+        nc.sync.dma_start(x_sb[:], x)
+        w_sb = held.tile([K, E, M], BF16, name="w_sb")
+        nc.sync.dma_start(w_sb[:], w.rearrange("e k m -> k e m"))
+        w2_sb = held.tile([P, M_BLOCKS, O], BF16, name="w2_sb")
+        nc.sync.dma_start(w2_sb[:], w2.rearrange("(m p) o -> p m o", p=P))
+        bias_sb = held.tile([P, O_BLOCKS], F32, name="bias_sb")
+        nc.scalar.dma_start(bias_sb[:], b.rearrange("(a p) o -> p (a o)", p=P))
+
+        identity = held.tile([P, P], BF16, name="identity")
+        make_identity(nc, identity[:])
+
+        windows = [psum.tile([P, S], F32, name=f"window{m}") for m in range(M_BLOCKS)]
+        for m in range(M_BLOCKS):
+            nc.tensor.matmul(windows[m][:], identity[:], base_sb[:, m, :], start=True, stop=False)
+
+        for m in range(M_BLOCKS):
+            for e in range(E):
+                piece = offsets[:, e * LIST_COLUMNS : (e + 1) * LIST_COLUMNS]
+                nc.tensor.matmul(
+                    windows[m][:].indirect(piece),
+                    w_sb[:, e, m * P : (m + 1) * P],
+                    x_sb[:, e * Q : (e + 1) * Q],
+                    start=False,
+                    stop=e == E - 1,
+                )
+
+        z_sb = [held.tile([P, S], BF16, name=f"z{m}") for m in range(M_BLOCKS)]
+        for m in range(M_BLOCKS):
+            if m % 2 == 0:
+                nc.vector.tensor_copy(z_sb[m][:], windows[m][:])
+            else:
+                nc.scalar.copy(z_sb[m][:], windows[m][:])
+
+        y = [psum.tile([P, S], F32, name=f"y{o}") for o in range(O_BLOCKS)]
+        for m in range(M_BLOCKS):
+            for o in range(O_BLOCKS):
+                nc.tensor.matmul(
+                    y[o][:],
+                    w2_sb[:, m, o * P : (o + 1) * P],
+                    z_sb[m][:],
+                    start=m == 0,
+                    stop=m == M_BLOCKS - 1,
+                )
+
+        for o in range(O_BLOCKS):
+            out_sb = held.tile([P, S], F32, name=f"out_sb{o}")
+            nc.scalar.activation(out_sb[:], y[o][:], GELU_TANH, bias=bias_sb[:, o : o + 1])
+            nc.sync.dma_start(out[o * P : (o + 1) * P, :], out_sb[:])

@@ -16,6 +16,7 @@ N = E * Q
 O = 256
 M_BLOCKS = M // P
 O_BLOCKS = O // P
+WARM_UPS = 6
 LIST_COLUMNS = Q // 16
 
 FLOPS = 2 * K * N * M + 2 * M * O * S
@@ -40,6 +41,15 @@ def tile_rows_thenproj_gelu_kernel(tc, base, x, w, w2, b, offs, out):
         nc.sync.dma_start(w2_sb[:], w2.rearrange("(m p) o -> p m o", p=P))
         bias_sb = held.tile([P, O_BLOCKS], F32, name="bias_sb")
         nc.scalar.dma_start(bias_sb[:], b.rearrange("(a p) o -> p (a o)", p=P))
+
+        zeros = held.tile([P, S], BF16, name="zeros")
+        nc.vector.memset(zeros[:], 0.0)
+        early_gelu = held.tile([P, 1], F32, name="early_gelu")
+        nc.scalar.activation(early_gelu[:], zeros[:, 0:1], GELU_TANH)
+
+        warm = psum.tile([P, S], F32, name="warm")
+        for i in range(WARM_UPS):
+            nc.tensor.matmul(warm[:], zeros[:, 0:P], zeros[:], start=True, stop=True)
 
         identity = held.tile([P, P], BF16, name="identity")
         make_identity(nc, identity[:])

@@ -16,7 +16,7 @@ N = E * Q
 O = 256
 M_BLOCKS = M // P
 O_BLOCKS = O // P
-WARM_UPS = 6
+WARM_UPS = 3
 LIST_COLUMNS = Q // 16
 
 FLOPS = 2 * K * N * M + 2 * M * O * S
@@ -40,7 +40,7 @@ def tile_rows_thenproj_gelu_kernel(tc, base, x, w, w2, b, offs, out):
         w2_sb = held.tile([P, M_BLOCKS, O], BF16, name="w2_sb")
         nc.sync.dma_start(w2_sb[:], w2.rearrange("(m p) o -> p m o", p=P))
         bias_sb = held.tile([P, O_BLOCKS], F32, name="bias_sb")
-        nc.scalar.dma_start(bias_sb[:], b.rearrange("(a p) o -> p (a o)", p=P))
+        nc.sync.dma_start(bias_sb[:], b.rearrange("(a p) o -> p (a o)", p=P))
 
         zeros = held.tile([P, S], BF16, name="zeros")
         nc.vector.memset(zeros[:], 0.0)

@@ -17,6 +17,8 @@ O = 256
 M_BLOCKS = M // P
 O_BLOCKS = O // P
 WARM_UPS = 3
+HALVES = 2
+HALF = S // HALVES
 LIST_COLUMNS = Q // 16
 
 FLOPS = 2 * K * N * M + 2 * M * O * S
@@ -69,25 +71,29 @@ def tile_rows_thenproj_gelu_kernel(tc, base, x, w, w2, b, offs, out):
                     stop=e == E - 1,
                 )
 
-        z_sb = [held.tile([P, S], BF16, name=f"z{m}") for m in range(M_BLOCKS)]
+        halves = [slice(h * HALF, (h + 1) * HALF) for h in range(HALVES)]
+        z_sb = [[held.tile([P, HALF], BF16, name=f"z{m}_{h}") for h in range(HALVES)] for m in range(M_BLOCKS)]
         for m in range(M_BLOCKS):
-            if m % 2 == 0:
-                nc.vector.tensor_copy(z_sb[m][:], windows[m][:])
-            else:
-                nc.scalar.copy(z_sb[m][:], windows[m][:])
+            for h in range(HALVES):
+                if m % 2 == 0:
+                    nc.vector.tensor_copy(z_sb[m][h][:], windows[m][:, halves[h]])
+                else:
+                    nc.scalar.copy(z_sb[m][h][:], windows[m][:, halves[h]])
 
-        y = [psum.tile([P, S], F32, name=f"y{o}") for o in range(O_BLOCKS)]
-        for m in range(M_BLOCKS):
+        y = [[psum.tile([P, HALF], F32, name=f"y{o}_{h}") for h in range(HALVES)] for o in range(O_BLOCKS)]
+        for h in range(HALVES):
+            for m in range(M_BLOCKS):
+                for o in range(O_BLOCKS):
+                    nc.tensor.matmul(
+                        y[o][h][:],
+                        w2_sb[:, m, o * P : (o + 1) * P],
+                        z_sb[m][h][:],
+                        start=m == 0,
+                        stop=m == M_BLOCKS - 1,
+                    )
+
+        for h in range(HALVES):
             for o in range(O_BLOCKS):
-                nc.tensor.matmul(
-                    y[o][:],
-                    w2_sb[:, m, o * P : (o + 1) * P],
-                    z_sb[m][:],
-                    start=m == 0,
-                    stop=m == M_BLOCKS - 1,
-                )
-
-        for o in range(O_BLOCKS):
-            out_sb = held.tile([P, S], F32, name=f"out_sb{o}")
-            nc.scalar.activation(out_sb[:], y[o][:], GELU_TANH, bias=bias_sb[:, o : o + 1])
-            nc.sync.dma_start(out[o * P : (o + 1) * P, :], out_sb[:])
+                out_sb = held.tile([P, HALF], F32, name=f"out_sb{o}_{h}")
+                nc.scalar.activation(out_sb[:], y[o][h][:], GELU_TANH, bias=bias_sb[:, o : o + 1])
+                nc.sync.dma_start(out[o * P : (o + 1) * P, halves[h]], out_sb[:])

import concourse.mybir as mybir
from concourse.masks import make_identity

BF16 = mybir.dt.bfloat16
F32 = mybir.dt.float32
U16 = mybir.dt.uint16
GELU_TANH = mybir.ActivationFunctionType.Gelu_apprx_tanh

P = 128
S = 512
K = 128
M = 384
E = 2
Q = 64
N = E * Q
O = 256
M_BLOCKS = M // P
O_BLOCKS = O // P
WARM_UPS = 3
HALVES = 2
HALF = S // HALVES
LIST_COLUMNS = Q // 16

FLOPS = 2 * K * N * M + 2 * M * O * S


def tile_rows_thenproj_gelu_kernel(tc, base, x, w, w2, b, offs, out):
    nc = tc.nc
    with (
        tc.tile_pool(name="held", bufs=1) as held,
        tc.psum_pool(name="psum", bufs=1) as psum,
    ):
        base_sb = held.tile([P, M_BLOCKS, S], BF16, name="base_sb")
        for m in range(M_BLOCKS):
            nc.sync.dma_start(base_sb[:, m, :], base[m * P : (m + 1) * P, :])
        offsets = held.tile([P, N // 16], U16, name="offsets")
        nc.sync.dma_start(offsets[:], offs)
        x_sb = held.tile([K, N], BF16, name="x_sb")
        nc.sync.dma_start(x_sb[:], x)
        w_sb = held.tile([K, E, M], BF16, name="w_sb")
        nc.sync.dma_start(w_sb[:], w.rearrange("e k m -> k e m"))
        w2_sb = held.tile([P, M_BLOCKS, O], BF16, name="w2_sb")
        nc.sync.dma_start(w2_sb[:], w2.rearrange("(m p) o -> p m o", p=P))
        bias_sb = held.tile([P, O_BLOCKS], F32, name="bias_sb")
        nc.sync.dma_start(bias_sb[:], b.rearrange("(a p) o -> p (a o)", p=P))

        zeros = held.tile([P, S], BF16, name="zeros")
        nc.vector.memset(zeros[:], 0.0)
        early_gelu = held.tile([P, 1], F32, name="early_gelu")
        nc.scalar.activation(early_gelu[:], zeros[:, 0:1], GELU_TANH)

        warm = psum.tile([P, S], F32, name="warm")
        for i in range(WARM_UPS):
            nc.tensor.matmul(warm[:], zeros[:, 0:P], zeros[:], start=True, stop=True)

        identity = held.tile([P, P], BF16, name="identity")
        make_identity(nc, identity[:])

        windows = [psum.tile([P, S], F32, name=f"window{m}") for m in range(M_BLOCKS)]
        for m in range(M_BLOCKS):
            nc.tensor.matmul(windows[m][:], identity[:], base_sb[:, m, :], start=True, stop=False)

        for m in range(M_BLOCKS):
            for e in range(E):
                piece = offsets[:, e * LIST_COLUMNS : (e + 1) * LIST_COLUMNS]
                nc.tensor.matmul(
                    windows[m][:].indirect(piece),
                    w_sb[:, e, m * P : (m + 1) * P],
                    x_sb[:, e * Q : (e + 1) * Q],
                    start=False,
                    stop=e == E - 1,
                )

        halves = [slice(h * HALF, (h + 1) * HALF) for h in range(HALVES)]
        z_sb = [[held.tile([P, HALF], BF16, name=f"z{m}_{h}") for h in range(HALVES)] for m in range(M_BLOCKS)]
        for m in range(M_BLOCKS):
            for h in range(HALVES):
                if m % 2 == 0:
                    nc.vector.tensor_copy(z_sb[m][h][:], windows[m][:, halves[h]])
                else:
                    nc.scalar.copy(z_sb[m][h][:], windows[m][:, halves[h]])

        y = [[psum.tile([P, HALF], F32, name=f"y{o}_{h}") for h in range(HALVES)] for o in range(O_BLOCKS)]
        for h in range(HALVES):
            for m in range(M_BLOCKS):
                for o in range(O_BLOCKS):
                    nc.tensor.matmul(
                        y[o][h][:],
                        w2_sb[:, m, o * P : (o + 1) * P],
                        z_sb[m][h][:],
                        start=m == 0,
                        stop=m == M_BLOCKS - 1,
                    )

        for h in range(HALVES):
            for o in range(O_BLOCKS):
                out_sb = held.tile([P, HALF], F32, name=f"out_sb{o}_{h}")
                nc.scalar.activation(out_sb[:], y[o][h][:], GELU_TANH, bias=bias_sb[:, o : o + 1])
                nc.sync.dma_start(out[o * P : (o + 1) * P, halves[h]], out_sb[:])
